import numpy as np, ml_dtypes
CORES = [25,29,65,69,153,157,193,197]
N = 8
BF = ml_dtypes.bfloat16
W, M, C, R, P = 2048, 1280, 256, 2, 4
def accounts(rng):
    H = W // 2; k = np.stack([rng.permutation(H) for _ in range(8)]); pw = rng.choice(np.array([1.0, 1.5, 2.0]), 8)
    c = np.minimum((H * rng.random((N, 8, 16 * M)) ** pw[None, :, None]).astype(np.int64), H - 1)
    e = (2 * k[np.arange(8)[None, :, None], c] + rng.integers(0, 2, c.shape)).reshape(N, 8, 16, M)
    none = (rng.random((N, 8, 16, M)) < 0.6 * rng.random((N, 8, 1, M)) ** 2) | (rng.random((N, 8, 1, M)) < 0.01)
    return np.where(none, W, e)
def keeps(rng):
    return rng.choice(np.array([0.0, 0.1, 0.3, 0.8]), (N, 8, 1, W // 2))
def books(rng, acct, keep):
    H = W // 2; out = rng.integers(0, M, (N, 8, 16, H)); m = np.tile(np.arange(M), 16)
    for q in range(N):
        for g in range(8):
            o = rng.permutation(16 * M); c = acct[q, g].reshape(-1)[o] >> 1
            s = np.argsort(c, kind="stable"); c = c[s]; who = m[o[s]]
            pos = np.arange(16 * M) - np.searchsorted(c, c)
            ok = (pos < 16) & (c < H) & (rng.random(16 * M) < keep[q, g, 0][np.minimum(c, H - 1)])
            out[q, g, pos[ok], c[ok]] = who[ok]
    return np.take_along_axis(out, np.argsort(rng.random(out.shape), axis=2), 2)
def losses(rng):
    return np.clip(np.rint(90 * rng.standard_normal((N, 8, 16, W), dtype=np.float32)), -255, 255).astype(np.int64)
def tops(loss, acct):
    x = np.take_along_axis(np.concatenate([loss, np.zeros((N, 8, 16, 1), np.int64)], axis=3), acct[..., :R * C].reshape(N, 8, 1, -1), 3)
    return np.max(np.add.reduce(x.reshape(N, 8, 16, 16, R * C), axis=3), axis=2)
def pack(loss, acct, book, cap):
    return {"loss": np.ascontiguousarray(loss.reshape(N, 128, W)).astype(np.float32).astype(BF), "acct": np.ascontiguousarray(acct.reshape(N, 128, M)).astype(np.int32),
            "book": np.ascontiguousarray(book.reshape(N, 128, W // 2)).astype(np.int32), "cap": np.ascontiguousarray(cap).astype(np.int32)}
def setup_inputs(rng):
    acct = accounts(rng)
    return pack(losses(rng), acct, books(rng, acct, keeps(rng)), rng.integers(0, 900, (N, 8, R * C)))
def setup_inputs_ties(rng):
    acct = accounts(rng); acct[:, ::2, 8:12] = acct[:, ::2, 0:4]
    loss = rng.integers(-2, 3, (N, 8, 16, W)) * rng.choice(np.array([1, 3, 100]), (N, 8, 1, 1)); loss[:, 1::2, 8:] = loss[:, 1::2, :8]
    loss[:, 6] = rng.integers(180, 255, (N, 1, 1)) + rng.integers(-1, 2, (N, 16, W))
    cap = np.clip(tops(loss, acct) + rng.choice(np.array([-1, -1, 0, 1]), (N, 8, R * C)), 0, 4095)
    keep = keeps(rng); keep[:, 6] = 0.8
    return pack(loss, acct, books(rng, acct, keep), cap)
def setup_inputs_crowd(rng):
    H = W // 2; acct = accounts(rng); loss = losses(rng); cap = rng.integers(0, 900, (N, 8, R * C))
    acct[:, 2:4] = 2 * rng.permutation(H)[:64][rng.integers(0, 64, (N, 2, 16, M))] + rng.integers(0, 2, (N, 2, 16, M))
    loss[:, :2] = rng.integers(-15, 16, (N, 2, 16, W)); cap[:, :2] = 0
    x = [int(2 * rng.integers(0, H)), int(2 * rng.integers(0, H) + 1)]; y = np.zeros((N, 2, 16), np.int64)
    for g in range(2):
        loss[:, g, :, x[g]] = 255
        for q in range(N):
            y[q, g] = R * C + rng.permutation(M - R * C)[:16]
            acct[q, g, rng.integers(0, 16, R * C), np.arange(R * C)] = x[g]
            acct[q, g, rng.integers(0, 16, 16), y[q, g]] = x[g] ^ 1
            acct[q, g, :, y[q, g, 1]] = x[g] ^ 1
    k = rng.permutation(H); e = 2 * k[:R * C] + rng.integers(0, 2, R * C); v = np.zeros((N, R * C), np.int64)
    acct[:, 4] = np.where(acct[:, 4] == W, W, 2 * k[rng.integers(R * C, H, (N, 16, M))] + rng.integers(0, 2, (N, 16, M)))
    big = rng.integers(-15, 16, (N, 16, W)); big[:, :, e] = rng.integers(240, 256, (N, 16, R * C)); loss[:, 4] = big; cap[:, 4] = 0
    for q in range(N):
        v[q] = R * C + rng.permutation(M - R * C)[:R * C]
        acct[q, 4, rng.integers(0, 16, R * C), np.arange(R * C)] = e
        acct[q, 4, rng.integers(0, 16, R * C), v[q]] = e ^ 1
    book = books(rng, acct, keeps(rng))
    for g in range(2):
        for q in range(N):
            book[q, g, :, x[g] >> 1] = y[q, g]; book[q, g, 0, x[g] >> 1] = rng.integers(0, R * C)
    for q in range(N): book[q, 4, rng.integers(0, 16, R * C), e >> 1] = v[q]
    return pack(loss, acct, book, cap)
def setup_inputs_ends(rng):
    H = W // 2; acct = accounts(rng); loss = losses(rng); cap = rng.integers(0, 300, (N, 8, R * C))
    acct[:, 0] = rng.choice(np.array([0, 1, W - 2, W - 1, W]), (N, 16, M))
    acct[:, 1, :, ::2] = acct[:, 1, :1, ::2]
    acct[:, 2:4, :, M - 1] = W
    acct[:, 4] = 2 * (rng.integers(-16, 16, (N, 16, M)) % H) + rng.integers(0, 2, (N, 16, M))
    acct[:, 5, 1:] = W
    acct[:, 6] = np.where(acct[:, 6] == W, rng.integers(0, W, (N, 16, M)), acct[:, 6]); loss[:, 6, 15] = 255
    cap[:, 6] = rng.choice(np.array([0, 4079, 4080, 4095]), (N, R * C))
    loss[:, 7, 1:] = -255
    book = books(rng, acct, np.full((N, 8, 1, H), 0.8))
    book[:, 2:4, :15] = M - 1
    book[:, 4] = rng.choice(np.array([0, M - 1, C - 1, C]), (N, 16, H))
    return pack(loss, acct, book, cap)
def setup_inputs_quiet(rng):
    acct = accounts(rng); cap = rng.integers(0, 900, (N, 8, R * C)); keep = keeps(rng); q = rng.permutation(N); g = rng.permutation(8)
    cap[q[0]] = 4095; cap[q[0], g[0]] = rng.integers(0, 300, R * C); cap[q[1]] = 0; cap[:, g[1]] = 4095
    keep[q[2]] = 0.0; keep[q[3]] = 1.0
    return pack(losses(rng), acct, books(rng, acct, keep), cap)
def setup_inputs_spread(rng):
    acct = rng.integers(0, W + 1, (N, 8, 16, M))
    loss = np.clip(np.rint(rng.standard_normal((N, 8, 16, W)) * np.exp2(rng.integers(0, 9, (N, 8, 1, W))) * (rng.random((N, 8, 1, W)) > 0.0625)), -255, 255).astype(np.int64)
    cap = np.exp2(12 * rng.random((N, 8, R * C))).astype(np.int64) - 1
    return pack(loss, acct, books(rng, acct, rng.random((N, 8, 1, W // 2))), cap)
def check_inputs(d):
    bad = []; v = np.asarray(d["loss"]).astype(np.float32)
    if not np.all((v >= -255) & (v <= 255) & (v == np.rint(v))): bad.append("whole numbers of loss")
    for k, hi in (("acct", W), ("book", M - 1), ("cap", 4095)):
        if np.min(d[k]) < 0 or np.max(d[k]) > hi: bad.append("range of " + k)
    return bad
def reference(loss, acct, book, cap):
    L = loss.astype(np.float32).astype(np.int64).reshape(N, 8, 16, W)
    L = np.concatenate([L, np.zeros((N, 8, 16, 1), np.int64)], axis=3)
    A = acct.astype(np.int64).reshape(N, 8, 16, M); B = book.astype(np.int64).reshape(N, 8, 16, W // 2); K = cap.astype(np.int64)
    said = np.zeros((N, 8, R * C), np.float32); slot = np.arange(C); rank = np.arange(N)[:, None]
    for t in range(R):
        lo = C * t
        mine = np.ascontiguousarray(A[..., lo:lo + C])
        x = np.take_along_axis(L, mine.reshape(N, 8, 1, 16 * C), 3).reshape(N, 8, 16, 16, C)
        z = np.add.reduce(x, axis=3)
        w = np.argmax(z, axis=2)
        over = np.max(z, axis=2) > K[..., lo:lo + C]
        xw = np.take_along_axis(x, w[:, :, None, None, :], 2)[:, :, 0]
        i = np.argmax(xw, axis=2)
        e = np.take_along_axis(mine, i[:, :, None], 2)[:, :, 0]
        d = 1 + (P * t + slot // (C // P)) % (N - 1)
        src = (rank - d) % N
        ok = over[src, :, slot].transpose(0, 2, 1)
        eo = np.where(ok, e[src, :, slot].transpose(0, 2, 1), 0); opp = eo ^ 1
        cand = np.take_along_axis(B, (eo >> 1)[:, :, None], 3)
        held = np.take_along_axis(A, cand.reshape(N, 8, 1, 16 * C), 3).reshape(N, 8, 16, 16, C)
        holds = np.any(held == opp[:, :, None, None], axis=2)
        found = ok & np.any(holds, axis=2)
        h = np.take_along_axis(cand, np.argmax(holds, axis=2)[:, :, None], 2)[:, :, 0]
        h = np.where(found, h, M + slot)
        same = (h[..., :, None] == h[..., None, :]) & (slot[None, :] < slot[:, None])
        acc = found & ~np.any(same, axis=-1)
        col = np.take_along_axis(A, np.where(acc, h, 0)[:, :, None], 3); new = np.where(col == opp[:, :, None], W, col)
        A = np.concatenate([A, np.zeros((N, 8, 16, C), np.int64)], axis=3)
        np.put_along_axis(A, np.ascontiguousarray(np.broadcast_to(np.where(acc, h, M + slot)[:, :, None], new.shape)), new, 3)
        A = np.ascontiguousarray(A[..., :M])
        back = acc[(rank + d) % N, :, slot].transpose(0, 2, 1)
        hit = back[:, :, None] & (np.arange(16)[None, None, :, None] == i[:, :, None])
        A[..., lo:lo + C] = np.where(hit, W, A[..., lo:lo + C])
        said[..., lo:lo + C] = over.astype(np.int64) + back.astype(np.int64)
    return {"left": (A < W).reshape(N, 128, M).astype(np.float32).astype(BF), "said": said}

from concourse.bass import DstId, RemoteDMATransfer
from concourse.mybir import AluOpType as A, ActivationFunctionType as F

BIG = 4096.0
f32, bf, h16, i32, u16 = "float32", "bfloat16", "float16", "int32", "uint16"
SCRATCH = {}
for _d, _l in (
    (bf, "L:2064 F16:16,16 W:16,8,16 Ib0:160 Ib1:160 Ib:128 I2:128 Ip:128 In:128 M0:144 oneB:128 negB:128 D0:256 dq0:256 dq:256 "
         "I16:256 gt:256 da:256 db:256 d1:256 Cst:256 Z:256 x0:4096 x1:4096 xT0:4100 xT1:4100 ohm:256 oa:256 over:256 eqJ:4096 "
         "eqD:256 eqO:1920 acc0:256 acc1:256 vb0:256 vb1:256 rem:8,2,16 k2:256 al:256 w1:256 leftS:1280 rv:256"),
    (i32, "aI:1280 Bk:1032 capI:32 pI:4 ci:8 ofi:96 s1:16 s2:16 ki:16 ea:16 eb:16 Es0:32 Es1:32 Ein0:32 Ein1:32 vl:16 vo:16 vc:16 ro:32"),
    (f32, "capF:32 capX:32 zin0:256 zin1:256 cf:24 xrow:160 grow:128 gmask:8 Ipad:160 fri:256 sl0:16 slotc:16 addX:256 "
          "zk:256 zc:256 kx:256 kT:256 ks:256 Aw:1536 Pm:1536 cT:256 held:4096 rep0:512 rep1:512 sc:256 t16:16 oppS:256 nS:256 yy:256 "
          "yT:256 dd:256 ab:336 nh:16 mm:256 nw:256 saidS:512"),
    (h16, "Ih0:160 Ih1:160 oneH:128 R:256 R2:256 a16:16,2,16 candp:256 candq:8,2,16 fst:256 sel:256 hH:256"),
    (u16, "ofu:96 offA0:256 offA1:256 off2:16 offB:16 offH:256 offS:16 offP:16"),
):
    for _w in _l.split():
        SCRATCH[_w.split(":")[0]] = ("sbuf", [128] + [int(_x) for _x in _w.split(":")[1].split(",")], _d)
for _k in range(8):
    SCRATCH["P%d" % _k] = ("psum", [128, 16, 32] if _k in (2, 7) else [128, 512], f32)
SEMAPHORES = ["ev", "ea", "et", "ep", "l0", "l1", "l2", "l3", "l4", "s0", "s1", "s2", "s3", "s4", "sent",
              "oD0", "oR0", "oD1", "oR1", "vb0", "vb1", "rl0", "rl1", "rl2", "rl3"]
NR = 8
NV = 9


def dist(t, b):
    return 1 + (4 * t + b) % (NR - 1)


def bits(engs):
    return sum(1 << e for e in engs)


def xpos(q):
    return 2 + 256 * q + 2 * (q // 8)


def work_order(T, topo, core, t):
    r = T.rank_of(core)
    D = [b for b in range(4) if topo.may_write(T.cores[(r - dist(t, b)) % NR], core)]
    b0 = [b for b in D if (b - 1) % 4 not in D][0]
    return [(b0 + k) % 4 for k in range(4)], len(D)


def routes(T, topo):
    first, second, count, relay = {}, {}, {}, {}
    for ph in range(4):
        for r in range(NR):
            src = T.cores[r]
            used, nrel, plan, out = [], 0, [], []
            for b in range(4):
                dst = T.cores[(r + dist(ph // 2, b) * (1 if ph % 2 == 0 else -1)) % NR]
                if topo.may_write(src, dst):
                    plan.append((dst, b, None, dst))
                else:
                    ports = [c for c in topo.cores_of(src)
                             if c not in T.cores and topo.die(c) == topo.die(src) and topo.may_write(c, dst)]
                    c = ports[nrel % len(ports)]
                    nrel += 1
                    lst = second.setdefault((ph, c), [])
                    plan.append((c, b, len(lst), dst))
                    lst.append((dst, b))
            plan.sort(key=lambda w: len(topo.engines(src, w[0])))
            for to, b, slot, dst in plan:
                engs = [e for e in topo.engines(src, to) if e not in used][:4]
                used += engs
                out.append((to, b, engs, slot, dst))
                key = (ph, to, "rl" if slot is not None else "D")
                count[key] = count.get(key, 0) + len(engs)
            first[(ph, src)] = out
    for (ph, c), lst in second.items():
        relay[(ph, c)] = []
        for k, (dst, b) in enumerate(lst):
            engs = topo.engines(c, dst)
            n = len(engs) // len(lst)
            relay[(ph, c)].append((dst, b, engs[k * n:(k + 1) * n], k))
            count[(ph, dst, "R")] = count.get((ph, dst, "R"), 0) + n
    return first, relay, count


def landing(T, topo, ph, b, dst):
    t = ph // 2
    if ph % 2 == 0:
        p = work_order(T, topo, dst, t)[0].index(b)
        return T["Ein%d" % t][:, 8 * p:8 * p + 8]
    return T["vb%d" % t][:, 64 * b:64 * b + 64]


def relay_slot(T, ph, k):
    n = (ph // 2) * 2 + k
    return T.ro[:, 8 * n:8 * n + 8] if ph % 2 == 0 else T.rv[:, 64 * n:64 * n + 64]


def arrival(ph, kind):
    return "o%s%d" % (kind, ph // 2) if ph % 2 == 0 else "vb%d" % (ph // 2)


def relay_program(g, core, T, topo, relay, count):
    sent = 0
    for ph in range(4):
        if (ph, core) not in relay:
            continue
        g.wait_ge(T.sem["rl%d" % ph], count[(ph, core, "rl")])
        tr = []
        for dst, b, engs, k in relay[(ph, core)]:
            rid, pid = topo.addr(dst, core)
            tr.append(RemoteDMATransfer(dst_ids=[DstId(rid=rid, pnc=pid)], dma_engine_mask=bits(engs), remote_sem=T.sem[arrival(ph, "R")],
                                        src=relay_slot(T, ph, k), dst=landing(T, topo, ph, b, dst)))
            sent += len(engs)
        g.remote_dma_fused(tr, local_sem=T.sem.sent)
    if sent:
        g.wait_ge(T.sem.sent, sent)


def rank_program(g, core, T, topo):
    first, relay, count = routes(T, topo)
    if T.rank_of(core) is None:
        relay_program(g, core, T, topo, relay, count)
        return
    ops, hist, needed, stores, sent = [], {}, set(), [], [0]
    Q = {"v": g.vector, "a": g.scalar, "t": g.tensor, "p": g, "s": g.sync}
    ALL = slice(None)

    def V(name, *idx, parts=ALL):
        shape = SCRATCH[name][1][1:]
        lo, hi, stride = 0, 0, 1
        full = list(idx) + [ALL] * (len(shape) - len(idx))
        for d in reversed(range(len(shape))):
            r = range(shape[d])[full[d]]
            a, b = (r, r) if isinstance(r, int) else (r[0], r[-1])
            lo, hi, stride = lo + a * stride, hi + b * stride, stride * shape[d]
        return (T[name][(parts,) + tuple(idx)], [(name, lo, hi + 1)], [])

    def C(name, a, b=None, step=None):
        return V(name, slice(a, a + 1 if b is None else b, step))

    def IND(win, off):
        return (win[0].indirect(off[0]), win[1], off[1])

    def rec(eng, fn, outs, ins, token=None):
        me = ("c", eng, len(ops)) if token is None else token
        rd = [r for v in ins for r in v[1] + v[2]] + [r for v in outs for r in v[2]]
        wr = [r for v in outs for r in v[1]]
        last = {}
        for kind, regs in (("r", rd), ("w", wr)):
            for name, lo, hi in regs:
                for k2, lo2, hi2, tok in hist.get(name, []):
                    same = tok[0] == "c" and tok[1] == eng and token is None
                    clash = lo < hi2 and lo2 < hi and (kind == "w" or k2 == "w")
                    if (clash and eng != "t") if same else (clash or SCRATCH[name][0] == "psum"):
                        if tok[1] not in last or last[tok[1]][2] < tok[2]:
                            last[tok[1]] = tok
        for kind, regs in (("r", rd), ("w", wr)):
            for name, lo, hi in regs:
                hist.setdefault(name, []).append((kind, lo, hi, me))
        ops.append((eng, fn, list(last.values()), token))

    def ext(view, sem, n):
        for name, lo, hi in view[1]:
            hist.setdefault(name, []).append(("w", lo, hi, ("s", sem, n)))

    def sv(x):
        return x[0] if isinstance(x, tuple) else x

    def ts(out, in0, s1, op0, s2=None, op1=None):
        more = () if op1 is None else (op1,)
        rec("v", lambda: g.vector.tensor_scalar(out[0], in0[0], sv(s1), sv(s2), op0, *more), [out],
            [in0] + [x for x in (s1, s2) if isinstance(x, tuple)])

    def tt(out, in0, in1, op):
        rec("v", lambda: g.vector.tensor_tensor(out[0], in0[0], in1[0], op), [out], [in0, in1])

    def cp(out, in_):
        rec("v", lambda: g.vector.tensor_copy(out[0], in_[0]), [out], [in_])

    def tr(out, in_):
        rec("v", lambda: g.vector.transpose(out[0], in_[0]), [out], [in_])

    def ms(out, c):
        rec("v", lambda: g.vector.memset(out[0], c), [out], [])

    def scan(out, d0, d1, op0, op1):
        rec("v", lambda: g.vector.tensor_tensor_scan(out[0], d0[0], d1[0], -20000.0, op0, op1), [out], [d0, d1])

    def act(out, in_, scale=1.0, bias=0.0, fn=F.Identity):
        rec("a", lambda: g.scalar.activation(out[0], in_[0], fn, bias=sv(bias), scale=sv(scale)), [out],
            [in_] + [x for x in (scale, bias) if isinstance(x, tuple)])

    def mm(out, lhsT, rhs, start, stop):
        rec("t", lambda: g.tensor.matmul(out[0], lhsT[0], rhs[0], start, stop), [out], [lhsT, rhs])

    def iota(out, pat, base, cm, fl=True):
        kw = {"allow_small_or_imprecise_dtypes": True} if fl else {}
        rec("p", lambda: g.iota(out[0], pat, base, cm, **kw), [out], [])

    def load(eng, out, src, sem):
        rec(eng, lambda: Q[eng].dma_start(out[0], src), [out], [], ("s", sem, 16))

    def store(eng, dst, in_, sem):
        rec(eng, lambda: Q[eng].dma_start(dst, in_[0]), [], [in_], ("s", sem, 16))
        stores.append((eng, sem))

    def send(ph, name):
        trs, w = [], 8 if ph % 2 == 0 else 64
        for to, b, engs, slot, dst in first[(ph, core)]:
            rid, pid = topo.addr(to, core)
            trs.append(RemoteDMATransfer(
                dst_ids=[DstId(rid=rid, pnc=pid)], dma_engine_mask=bits(engs),
                remote_sem=T.sem[arrival(ph, "D") if slot is None else "rl%d" % ph], src=T[name][:, w * b:w * b + w],
                dst=landing(T, topo, ph, b, dst) if slot is None else relay_slot(T, ph, slot)))
            sent[0] += len(engs)
        rec("p", lambda: g.remote_dma_fused(trs, local_sem=T.sem.sent), [], [V(name)], ("r", "sent", sent[0]))

    col = lambda k: C("cf", k)
    end16 = lambda name: C(name, 15, 256, 16)
    W256 = lambda name: C(name, 0, 256)
    IDN = lambda: C("Ipad", 16, 144)

    load("s", C("aI", 0, 256), T.acct[:, 0:256], "l0")
    load("a", V("capI"), T.cap[:], "l1")
    load("s", C("L", 0, 2048), T.loss[:], "l2")
    load("s", C("aI", 256, 1280), T.acct[:, 256:1280], "l3")
    load("s", C("Bk", 0, 1024), T.book[:], "l4")

    iota(C("pI", 0), [[0, 1]], 0, 1, False)
    iota(C("ofi", 0, 16), [[1, 16]], 0, 16, False)
    iota(V("dq0"), [[0, 16], [1, 16]], 0, 0)
    iota(V("xrow"), [[1, 160]], 0, 0)
    iota(C("ofi", 32, 64), [[8, 2], [1, 8], [16, 2]], 0, 0, False)
    iota(V("fri"), [[-1, 256]], 255, 0)
    iota(V("grow"), [[1, 8], [0, 16]], 0, 0)
    iota(V("Es0"), [[0, 32]], 0, 0, False)
    iota(V("Es1"), [[0, 32]], 0, 0, False)
    for a in (0, 2050):
        iota(C("xT0", a, a + 2), [[0, 2]], -1, 0)
        iota(C("xT1", a, a + 2), [[0, 2]], -1, 0)
    iota(C("Bk", 1024, 1032), [[0, 8]], 0, 0, False)
    iota(C("ofi", 16, 32), [[1, 16]], 0, 0, False)
    iota(C("ofi", 64, 80), [[64, 4], [4, 4]], 0, 0, False)
    iota(C("ofi", 80, 96), [[2, 16]], 0, 0, False)
    iota(V("sl0"), [[16, 16]], 256 - 2 * int(BIG), 0)
    iota(V("F16"), [[33, 16], [-33, 16]], 1, 0)
    rec("p", lambda: g.affine_select(T.F16[:], T.F16[:], [[-1, 16], [1, 16]], A.is_ge, 0.0, 0, 0), [V("F16")], [V("F16")])
    iota(V("Z"), [[0, 256]], 0, 0)
    iota(C("Aw", 0, 256), [[0, 256]], 0, 0)

    ts(C("ci", 0), C("pI", 0), 15, A.bitwise_and)
    ts(C("ci", 1), C("pI", 0), 4, A.logical_shift_right)
    ts(C("ci", 2), C("pI", 0), 4, A.logical_shift_right, 1, A.bitwise_and)
    ts(C("ci", 3), C("pI", 0), 3, A.bitwise_and)
    ts(C("ci", 4), C("pI", 0), 2, A.logical_shift_right, 3, A.bitwise_and)
    ts(C("ci", 5), C("pI", 0), 3, A.logical_shift_right, 1, A.bitwise_and)
    ts(C("ofi", 0, 16), C("ofi", 0, 16), 255, A.bitwise_and)
    cp(C("cf", 0, 6), C("ci", 0, 6))
    ts(col(15), C("pI", 0), 16.0, A.add)
    cp(C("ofu", 0, 16), C("ofi", 0, 16))
    ms(V("D0"), 0.0)
    ms(C("L", 2048, 2064), 0.0)
    for k, (src, a, b) in enumerate(((1, 16.0, 15.0), (2, -1.0, 1.0), (0, -1.0, 0.0), (0, 256.0, 257.0), (0, 1.0, -31.0),
                                     (0, -1.0 / 16, 15.0 / 16 + 1.0 / 65536), (2, 33554432.0, -33554432.0), (2, -33554432.0, 0.0))):
        act(col(6 + k), col(src), a, b)
    act(col(14), col(3), 16.0, col(4))
    act(col(16), col(5), 2.0, col(9))
    act(col(17), col(5), -2048.0, col(9))
    ts(V("Ipad"), V("xrow"), col(15), A.is_equal)
    ms(C("D0", 0, 256, 16), -67108864.0)
    ts(V("M0"), C("xrow", 0, 144), col(6), A.is_equal, BIG, A.mult)
    act(V("dq"), V("dq0"), 1.0, col(8))
    act(V("da"), V("dq"), fn=F.Abs)
    act(V("I16"), V("da"), -1.0, 1.0, F.Relu)

    def perm(t):
        cp(V("offA%d" % t), IND(C("aI", 256 * t, 256 * t + 256), C("ofu", 0, 16)))

    def zcap(t):
        act(V("zin%d" % t), IND(V("capX"), C("ofu", 32 + 16 * t, 48 + 16 * t)))

    def zinit(t):
        mm(W256("P0"), IDN(), V("fri"), True, False)
        mm(W256("P0"), IDN(), V("zin%d" % t), False, False)

    def xg(t, eng, q0, q1):
        (act if eng == "a" else cp)(C("x%d" % t, 256 * q0, 256 * q1), IND(V("L"), C("offA%d" % t, 16 * q0, 16 * q1)))

    def xt(t, q0, q1):
        tr(C("xT%d" % t, xpos(q0), xpos(q1 - 1) + 256), C("x%d" % t, 256 * q0, 256 * q1))
        for q in range(q0, q1):
            mm(W256("P0"), C("M0", 15 - q, 143 - q), C("xT%d" % t, xpos(q), xpos(q) + 256), False, q == 15)

    def swap(bank, r, mats, rhs, start, stop):
        for g2 in range(2):
            for c2 in range(2):
                s0 = 16 - 16 * (c2 - g2)
                mm(V(bank, r, slice(16 * g2, 16 * g2 + 16)), C(mats % g2, s0, s0 + 128), rhs(c2),
                   start and c2 == 0, stop and (c2 == 1 if start else g2 + c2 == 2))

    def places(t):
        r = slice(8 * t, 8 * t + 8)
        ts(V("a16", r), C("aI", 256 * t, 256 * t + 256), 1.0, A.add)
        if t == 1:
            mm(V("P2", slice(0, 8)), V("oneB"), V("Z"), True, False)
        swap("P2", slice(0, 8), "Ih%d", lambda c2: V("a16", r, c2, ALL), t == 0, t == 0)

    def addx():
        act(V("addX"), V("P2", slice(0, 8)), 1.0 / 65536, col(11))

    def offer_tail(t, z):
        scan(V("zk"), V("D0"), z, A.add, A.max)
        ts(V("s1"), end16("zk"), col(17), A.max)
        ts(V("s2"), V("s1"), 4095, A.bitwise_and)
        ts(V("off2"), V("s2"), -1.0, A.mult, col(16), A.add)
        tt(V("kx"), IND(V("xT%d" % t), V("off2")), V("addX"), A.add)
        tr(V("kT"), V("kx"))
        scan(V("ks"), V("D0"), V("kT"), A.add, A.max)
        ts(V("ki"), end16("ks"), 65536.0, A.mult, 2052.0, A.max)
        ts(V("ea"), V("ki"), 4094, A.bitwise_and)
        ts(V("eb"), V("ki"), 1, A.bitwise_and)
        tt(C("Es%d" % t, 0, 32, 2), V("ea"), V("eb"), A.subtract)
        send(2 * t, "Es%d" % t)

    def code_a():
        ts(V("vl"), V("ki"), 12, A.logical_shift_right, 15, A.bitwise_and)
        ts(V("vo"), V("ki"), 65536.0, A.is_ge, 16.0, A.mult)

    def code_b():
        tt(V("vc"), V("vl"), V("vo"), A.add)

    def code_c():
        tt(V("R2"), IND(V("vc"), C("ofu", 16, 32)), V("I16"), A.mult)

    def offered(t, bank):
        mm(W256(bank), V("oneH"), V("R2"), True, True)
        act(V("oa"), W256(bank), 1.0, col(10), F.Abs)
        act(V("over"), W256(bank), fn=F.Sign)
        if t == 1:
            act(V("ohm"), V("oa"), -0.5, 0.5, F.Relu)

    cp(C("ofu", 32, 64), C("ofi", 32, 64))
    ts(V("capF"), V("capI"), -BIG, A.mult)
    perm(0)
    tr(V("capX"), V("capF"))
    ts(V("Ih0"), V("Ipad"), col(7), A.mult)
    ts(V("Ih1"), V("Ipad"), col(2), A.mult)
    zcap(0)
    zinit(0)
    xg(0, "v", 0, 4)
    for q0, q1 in ((4, 8), (8, 12), (12, 15), (15, 16)):
        xg(0, "a", q0, q1)
    xt(0, 0, 4)
    places(0)
    xt(0, 4, 8)
    perm(1)
    xt(0, 8, 12)
    ts(V("gmask"), C("grow", 0, 128, 16), col(1), A.is_equal)
    ts(V("oneH"), V("grow"), col(1), A.is_equal)
    xt(0, 12, 15)
    xt(0, 15, 16)
    addx()
    ts(V("oneB"), V("grow"), col(1), A.is_equal)
    offer_tail(0, W256("P0"))

    iota(V("Pm"), [[0, 1536]], 2049, 0)
    zcap(1)
    for q0 in range(0, 12, 4):
        xg(1, "a", q0, q0 + 4)
    for m in range(5):
        act(V("W", ALL, m, ALL), V("F16"), C("gmask", m))
    cp(C("ofu", 80, 96), C("ofi", 80, 96))
    ts(C("ofu", 64, 80), C("ofi", 64, 80), col(14), A.add)
    cp(C("ofu", 16, 32), C("ofi", 16, 32))
    ts(C("Aw", 256, 1536), V("aI"), 1.0, A.add)
    zinit(1)
    places(1)
    xt(1, 0, 4)
    xt(1, 4, 8)
    for m in range(5, 8):
        ts(V("W", ALL, m, ALL), V("F16"), C("gmask", m), A.mult)

    def mid_constants():
        act(V("db"), V("I16"), BIG)
        act(V("gt"), V("dq"), fn=F.Relu)
        act(V("Ib"), IDN())
        act(V("gt"), V("gt"), fn=F.Sign)
        act(V("negB"), V("oneB"), -BIG)
        act(V("Cst"), V("gt"), -3 * BIG, 4 * BIG)
        act(end16("Cst"), end16("gt"), -6 * BIG, 4 * BIG)

    def late_constants():
        act(V("slotc"), V("sl0"), 1.0, col(0))
        act(V("Ib0"), V("Ipad"), col(12))
        act(V("Ib1"), V("Ipad"), col(13))

    def last_constants():
        act(V("I2"), IDN(), 2.0)
        act(V("Ip"), IDN(), 2 * BIG)
        act(V("In"), IDN(), -2 * BIG)

    def verdicts(t, fill):
        ph = 2 * t
        order, nd = work_order(T, topo, core, t)
        bank = ["P1", "P4", "P5", "P6"]
        ein = "Ein%d" % t
        ext(C(ein, 0, 8 * nd), arrival(ph, "D"), count[(ph, core, "D")])
        ext(C(ein, 8 * nd, 32), arrival(ph, "R"), count[(ph, core, "R")])

        def gap():
            if fill:
                fill.pop(0)()

        def prep(p0, p1):
            n, r = p1 - p0, slice(2 * p0, 2 * p1)
            ts(C("offB", 4 * p0, 4 * p1), C(ein, 8 * p0, 8 * p1, 2), 0.5, A.mult, -0.75, A.add)
            tt(C("R", 64 * p0, 64 * p1), IND(C(ein, 8 * p0, 8 * p1), C("ofu", 80, 80 + 4 * n)), C("I16", 0, 64 * n), A.mult)
            ts(C("candp", 64 * p0, 64 * p1), IND(V("Bk"), C("offB", 4 * p0, 4 * p1)), 512.0, A.add)
            cp(V("candq", r), C("candp", 64 * p0, 64 * p1))
            for p in [p1 - 1] + list(range(p0, p1 - 1)):
                for k in range(8):
                    mm(C(bank[p], 64 * k, 64 * k + 64), V("oneH"), C("R", 64 * p, 64 * p + 64), True, True)
                if p == p1 - 1:
                    swap("P7", r, "Ih%d", lambda c2: V("candq", r, c2, ALL), True, True)
            gap()
            tr(C("cT", 64 * p0, 64 * p1), V("P7", r))
            ts(C("offH", 64 * p0, 64 * p1), IND(C("cT", 64 * p0, 64 * p1), C("ofu", 64, 64 + 4 * n)), -256.0, A.add)

        def hg(p, h0=0, h1=2):
            act(C("held", 1024 * p + 512 * h0, 1024 * p + 512 * h1), IND(V("Aw"), C("offH", 64 * p + 32 * h0, 64 * p + 32 * h1)))

        def cmp(p, h, rep=None, first_=None, parts=1):
            a = 1024 * p + 512 * h
            if rep is None:
                for lo, hi in ((0, 512),) if parts == 1 else ((0, 384), (384, 512)):
                    tt(C("eqJ", a + lo, a + hi), C("held", a + lo, a + hi), C(bank[p], lo, hi), A.is_equal)
            else:
                tt(C("eqJ", a, a + 512), IND(V("Aw"), C("offH", 64 * p + 32 * h, 64 * p + 32 * h + 32)), V(rep), A.is_equal)
            one = h == 0 if first_ is None else first_
            for j in range(8):
                mm(C("P3", 64 * p, 64 * p + 64), V("W", 8 * h + j), C("eqJ", a + 64 * j, a + 64 * j + 64), one and j == 0, not one and j == 7)

        def opp(p, src):
            act(C("oppS", 64 * order[p], 64 * order[p] + 64), C(src, 0, 64))

        prep(0, nd)
        if nd == 2:
            act(V("rep0"), V(bank[1]))
            if t == 1:
                hg(1, 0, 1)
            hg(0)
            opp(1, "rep0")
            cmp(1, 1, "rep0", True)
            if t == 0:
                mid_constants()
                cmp(1, 0, "rep0", False)
            prep(2, 4)
            if t == 1:
                cmp(1, 0, None, False)
            hg(2, 0, 1)
            hg(2, 1, 2)
            hg(3, 0, 1)
            hg(3, 1, 2)
            rest, done = (0, 2, 3), (1, 0, 2, 3)
        else:
            act(V("rep0"), V(bank[0]))
            hg(0, 0, 1)
            opp(0, "rep0")
            cmp(0, 1, "rep0", True)
            cmp(0, 0, None, False)
            prep(1, 4)
            act(V("rep1"), V(bank[3]))
            hg(1)
            hg(2, 0, 1)
            hg(2, 1, 2)
            opp(3, "rep1")
            cmp(3, 0, "rep1")
            cmp(3, 1, "rep1")
            rest, done = (1, 2), (0, 3, 1, 2)
        hB, hC, S_, hA = bank[done[1]], bank[done[0]], bank[done[2]], bank[done[3]]
        for p in rest:
            if p == rest[1]:
                gap()
                mm(W256(hC), V("Ib"), V("Cst"), True, False)
            if p == rest[-1] and t == 0:
                xg(1, "a", 12, 16)
            cmp(p, 0)
            cmp(p, 1, parts=2 if p == rest[-1] else 1)
            opp(p, bank[p])
        mm(W256(S_), V("oneB"), V("Z"), True, False)
        if t == 0:
            late_constants()
        gap()
        ts(V("fst"), W256("P3"), 0.0, A.is_gt)
        tt(V("sel"), V("fst"), V("candp"), A.mult)
        a = 64 * order[0]
        parts = [(a, 256, 0)] + ([(0, a, 256 - a)] if a else [])
        for to, alone, stop in ((hB, True, True), (hC, False, True), (hA, True, True), (S_, False, False)):
            for k, (lo, hi, at) in enumerate(parts):
                mm(C(to, lo, hi), V("oneH"), C("sel", at, at + hi - lo), alone, alone or (stop and k == len(parts) - 1))
        gap()
        scan(V("sc"), W256(hB), V("d1"), A.max, A.add)
        cp(V("hH"), W256(hB))
        tt(V("eqD"), V("sc"), W256(hC), A.is_equal)
        mm(W256(S_), V("negB"), V("eqD"), False, False)
        act(V("nh"), end16("sc"), -1.0, -2 * BIG)
        at = [sum(240 - 16 * k for k in range(s)) for s in range(16)]
        for s in range(NV, 15):
            act(C("ab", at[s] - at[NV], at[s + 1] - at[NV]), C(hA, 16 * s + 16, 256), 1.0, C("nh", s), F.Abs)
        act(C("eqO", at[NV], at[15]), C("ab", 0, at[15] - at[NV]), -1.0, 1.0, F.Relu)
        for s in range(NV):
            ts(C("eqO", at[s], at[s + 1]), C("hH", 16 * s + 16, 256), C("sc", 16 * s + 15), A.subtract, 2 * BIG, A.is_equal)
        for s in list(range(NV - 3)) + list(range(NV, 15)) + [NV - 3, NV - 2, NV - 1]:
            mm(C(S_, 16 * s + 16, 256), V("negB"), C("eqO", at[s], at[s + 1]), False, s == NV - 1)
        if t == 1:
            ts(V("acc1"), W256(S_), 0.0, A.is_gt, 0.5, A.mult)
        scan(V("sc"), W256(S_), V("d1"), A.max, A.add)
        if t == 0:
            act(V("k2"), W256(S_), fn=F.Sign)
            act(V("acc0"), V("k2"), 0.5, 0.0, F.Relu)
        send(ph + 1, "acc%d" % t)
        offered(t, hA)
        tt(V("t16"), end16("sc"), V("slotc"), A.max)
        ts(V("offS"), V("t16"), 2 * BIG - 256, A.add)

    def strike(between):
        tt(V("dd"), IND(V("Aw"), V("offS")), V("oppS"), A.subtract)
        act(W256("ab"), V("dd"), fn=F.Abs)
        act(V("mm"), W256("ab"), -2049.0, 2049.0, F.Relu)
        between()
        tt(IND(V("Aw"), V("offS")), V("nw"), V("mm"), A.max)

    def back(t):
        ext(V("vb%d" % t), "vb%d" % t, count[(2 * t + 1, core, "D")] + count[(2 * t + 1, core, "R")])

    def say(t):
        c = slice(256 * t, 256 * t + 256)
        mm(W256("P3"), V("Ib"), V("over"), True, False)
        mm(W256("P3"), V("I2"), V("vb%d" % t), False, True)
        act(V("saidS", c), W256("P3"))
        store("a", T.said[:, c], V("saidS", c, parts=slice(0, 128, 16)), "s%d" % (4 * t))

    def f1():
        ts(V("da"), V("dq"), 0.0, A.is_lt, -2 * BIG, A.mult)
        code_a()

    def f2():
        tt(V("d1"), V("da"), V("db"), A.add)
        code_b()

    def f3():
        ts(end16("d1"), end16("d1"), -3 * BIG, A.add)
        xt(1, 8, 12)

    def f4():
        code_a()
        code_b()
        code_c()

    verdicts(0, [f1, f2, f3, code_c, lambda: xt(1, 12, 16)])
    cp(IND(V("Pm"), V("offS")), V("oppS"))
    tt(V("rem"), C("Aw", 512, 768), C("Pm", 512, 768), A.is_equal)
    mm(W256("P3"), V("oneB"), V("rem"), True, True)
    act(V("nS"), W256("P3"), BIG)
    swap("P2", slice(0, 8), "Ib%d", lambda c2: V("rem", ALL, c2, ALL), False, True)
    addx()
    act(V("nw"), IND(V("Aw"), V("offS")))
    last_constants()
    scan(V("sc"), C("Pm", 512, 768), V("d1"), A.max, A.add)
    ts(V("offP"), end16("sc"), 2 * BIG - 1, A.add)
    tt(V("yy"), IND(V("L"), V("offP")), V("nS"), A.mult)
    tr(V("yT"), V("yy"))
    tt(V("zc"), W256("P0"), V("yT"), A.subtract)
    offer_tail(1, V("zc"))
    back(0)
    mm(W256("P1"), V("In"), V("oa"), True, False)
    mm(W256("P1"), V("Ip"), V("vb0"), False, True)
    strike(f4)
    tt(C("Aw", 256, 512), C("Aw", 256, 512), W256("P1"), A.max)
    say(0)
    verdicts(1, [])
    back(1)
    strike(lambda: cp(V("nw"), IND(V("Aw"), V("offS"))))
    act(C("leftS", 512, 1280), C("Aw", 768, 1536), -1.0, 2049.0, F.Sign)
    ts(V("al"), C("Aw", 512, 768), 2049.0, A.is_lt)
    ts(C("leftS", 0, 256), C("Aw", 256, 512), 2049.0, A.is_lt)
    tt(V("w1"), V("al"), V("ohm"), A.subtract)
    store("s", T.left[:, 0:256], C("leftS", 0, 256), "s2")
    store("s", T.left[:, 512:1280], C("leftS", 512, 1280), "s1")
    tt(C("leftS", 256, 512), V("w1"), V("vb1"), A.is_gt)
    store("s", T.left[:, 256:512], C("leftS", 256, 512), "s3")
    say(1)

    seen, plan, val, n = {}, [], {}, {}
    for eng, fn, deps, token in ops:
        plan.append([d for d in deps if seen.get((eng, d[1]), -1) < d[2]])
        for d in plan[-1]:
            seen[(eng, d[1])] = d[2]
            if d[0] == "c":
                needed.add(d[2])
    for k, op in enumerate(ops):
        if k in needed:
            n[op[0]] = val[k] = n.get(op[0], 0) + 1
    for k, (eng, fn, deps, token) in enumerate(ops):
        for d in plan[k]:
            if d[0] == "c":
                Q[eng].wait_ge(T.sem["e" + d[1]], val[d[2]])
            else:
                Q[eng].wait_ge(T.sem[d[1]], d[2])
        ins = fn()
        if token is not None and token[0] == "s":
            ins.then_inc(T.sem[token[1]], 16)
        elif k in needed:
            ins.then_inc(T.sem["e" + eng], 1)
    for eng, sem in stores:
        Q[eng].wait_ge(T.sem[sem], 16)
    g.wait_ge(T.sem.sent, sent[0])
